import numpy as np
import ml_dtypes


def mxq(x, axis, fmt="e4m3"):
    dtype, down = {"e4m3": (ml_dtypes.float8_e4m3fn, 7), "e5m2": (ml_dtypes.float8_e5m2, 14)}[fmt]
    v = np.moveaxis(np.asarray(x, np.float32).astype(ml_dtypes.bfloat16).astype(np.float64), axis, -1)
    blocks = v.reshape(v.shape[:-1] + (-1, 32))
    amax = np.abs(blocks).max(-1, keepdims=True)
    byte = np.maximum(np.where(amax > 0, np.frexp(amax)[1] - 1 + 127, 0) - down, 1)
    scale = np.exp2(byte - 127.0)
    codes = (blocks / scale).astype(np.float32).astype(dtype).astype(np.float64)
    return np.moveaxis((codes * scale).reshape(v.shape), -1, axis)


WIDE = False


def mx_kscale(k):
    if not WIDE:
        return np.ones(k)
    levels = np.array([30, -30])
    if k % 512:
        return np.exp2(np.random.permutation(np.resize(levels, k // 32))).repeat(32)
    a = np.empty((k // 512, 16))
    for p in range(k // 512):
        a[p, :8] = np.random.permutation(np.resize(levels, 8))
        for g in range(8):
            far = levels[np.abs(levels - a[p, g]) >= 10]
            a[p, g + 8] = far[np.random.randint(len(far))]
    return np.exp2(a.ravel()).repeat(32)


def f64(x):
    return np.asarray(x).astype(np.float64)


def striped(idx):
    return np.tile(np.asarray(idx).reshape(-1, 16).T, (8, 1)).astype(np.uint16)


def unstriped(offs):
    return offs[:16].T.reshape(-1).astype(np.int64)


E2M1 = np.array([0.0, 0.5, 1.0, 1.5, 2.0, 3.0, 4.0, 6.0, -0.0, -0.5, -1.0, -1.5, -2.0, -3.0, -4.0, -6.0])


def pack_weight(w, fmt):
    k, n = w.shape
    w = f64(np.asarray(w, np.float32).astype(ml_dtypes.bfloat16)).reshape(k // 32, 32, n)
    amax = np.abs(w).max(1)
    if fmt in ("e4m3", "e5m2"):
        byte = np.frexp(amax)[1] - 1 + 127 - (7 if fmt == "e4m3" else 14)
    else:
        mant, ex = np.frexp(amax / 6.0)
        byte = np.where(mant > 0.5, ex, ex - 1) + 127
    byte = np.clip(np.where(amax > 0, byte, 1), 1, 254)
    scaled = (w * np.exp2(127.0 - byte)[:, None, :]).reshape(k, n).astype(np.float32)
    by_word = np.ascontiguousarray(scaled.reshape(k // 512, 128, 4, n).transpose(0, 1, 3, 2))
    if fmt in ("e4m3", "e5m2"):
        words = by_word.astype(ml_dtypes.float8_e4m3fn if fmt == "e4m3" else ml_dtypes.float8_e5m2).view(np.uint8)
    else:
        c = by_word.astype(ml_dtypes.float4_e2m1fn).view(np.uint8) & 0xF
        words = (c[..., 0::2] | (c[..., 1::2] << 4)).reshape(k // 512, 128, 2 * n)
    return np.ascontiguousarray(words), np.ascontiguousarray(byte.astype(np.uint8).reshape(k // 512, 16, n))


def unpack_weight(words, scales, fmt):
    g, _, n = scales.shape
    words = np.ascontiguousarray(words).reshape(g, 128, n, -1)
    if fmt in ("e4m3", "e5m2"):
        vals = words.view(ml_dtypes.float8_e4m3fn if fmt == "e4m3" else ml_dtypes.float8_e5m2).astype(np.float64)
    else:
        nib = np.empty((g, 128, n, 4), np.uint8)
        nib[..., 0::2] = words & 0xF
        nib[..., 1::2] = words >> 4
        vals = E2M1[nib]
    vals = vals * np.repeat(np.exp2(scales.astype(np.float64) - 127.0), 8, axis=1)[..., None]
    return vals.transpose(0, 1, 3, 2).reshape(g * 512, n)


def sigmoid(v):
    return 1.0 / (1.0 + np.exp(-v))


def sgn(shape):
    return np.random.uniform(0.5, 2.0, shape) * np.where(np.random.standard_normal(shape) < 0, -1.0, 1.0)


K, T, J, R, V, O, N, S, E = 512, 1024, 256, 512, 1024, 128, 256, 1024, 1024


def setup_inputs():
    n = np.random.standard_normal
    idx = np.random.permutation(V)[:R]
    idx2 = np.random.permutation(T)[:J]
    idx3 = np.random.permutation(J)[:O]
    idx4 = np.random.permutation(J)[:O]
    idx5 = np.random.permutation(J)[:O]
    idx6 = np.random.permutation(S)[:N]
    idx7 = np.random.permutation(E)[:O]
    fk = mx_kscale(K)
    fr = mx_kscale(R)
    xtp = pack_weight(n((K, T)) / fk[:, None], "e4m3")
    wtp = pack_weight(n((K, V)) * 1 / np.sqrt(K) * fk[:, None], "e2m1")
    vsp = pack_weight(n((R, S)) * 1 / np.sqrt(R) / fr[:, None], "e5m2")
    return {
        "xt_words": xtp[0],
        "xt_scales": xtp[1],
        "wt_words": wtp[0],
        "wt_scales": wtp[1],
        "sa": (np.random.uniform(0.5, 1.6, (R, 1)) * fr[:, None]).astype(np.float32),
        "sb": (np.random.uniform(0.5, 1.6, (R, 1)) * fr[:, None]).astype(np.float32),
        "sg": (sgn((R, 1))).astype(np.float32),
        "bg": (np.random.uniform(-2.0, 2.0, (R, 1))).astype(np.float32),
        "vs_words": vsp[0],
        "vs_scales": vsp[1],
        "offs": striped(idx),
        "offs2": striped(idx2),
        "offs3": striped(idx3),
        "offs4": striped(idx4),
        "offs5": striped(idx5),
        "offs6": striped(idx6),
        "offs7": striped(idx7),
    }


def reference(xt_words, xt_scales, wt_words, wt_scales, sa, sb, sg, bg, vs_words, vs_scales, offs, offs2, offs3, offs4, offs5, offs6, offs7):
    idx = unstriped(offs)
    idx2 = unstriped(offs2)
    idx3 = unstriped(offs3)
    idx4 = unstriped(offs4)
    idx5 = unstriped(offs5)
    idx6 = unstriped(offs6)
    idx7 = unstriped(offs7)
    xtu = unpack_weight(xt_words, xt_scales, "e4m3")
    wtu = unpack_weight(wt_words, wt_scales, "e2m1")
    vsu = unpack_weight(vs_words, vs_scales, "e5m2")
    wtidxg = wtu[:, idx]
    xtidx2g = xtu[:, idx2]
    a = wtidxg.T @ xtidx2g
    hid = np.abs(a[:, idx3] * f64(sa) - a[:, idx4] * f64(sb)) * sigmoid(a[:, idx5] * f64(sg) + f64(bg))
    vsidx6g = vsu[:, idx6]
    hidq = mxq(hid, 0, "e4m3")
    p = vsidx6g.T @ hidq
    y = np.zeros((N, E))
    y[:, idx7] = p
    return y

@@ -1,0 +1,162 @@
+from contextlib import ExitStack
+
+import concourse.mybir as mybir
+
+F32 = mybir.dt.float32
+BF16 = mybir.dt.bfloat16
+I32 = mybir.dt.int32
+U32 = mybir.dt.uint32
+U16 = mybir.dt.uint16
+U8 = mybir.dt.uint8
+E4M3X4 = mybir.dt.float8_e4m3fn_x4
+E5M2X4 = mybir.dt.float8_e5m2_x4
+E2M1X4 = mybir.dt.float4_e2m1fn_x4
+ACT = mybir.ActivationFunctionType
+ALU = mybir.AluOpType
+
+K, T, J, R, V, O, N, S, E = 512, 1024, 256, 512, 1024, 128, 256, 1024, 1024
+P = 128
+PACK = 4
+FLOPS = 2 * K * R * J + 2 * R * N * O
+
+
+def tile_list_gatedlarger_chosen_store_scattered_kernel(
+    tc, xt_words, xt_scales, wt_words, wt_scales, sa, sb, sg, bg, vs_words, vs_scales,
+    offs, offs2, offs3, offs4, offs5, offs6, offs7, out,
+):
+    nc = tc.nc
+    with ExitStack() as ctx:
+        lists = ctx.enter_context(tc.tile_pool(name="lists", bufs=1))
+        keep = ctx.enter_context(tc.tile_pool(name="keep", bufs=1))
+        psum = ctx.enter_context(tc.psum_pool(name="psum", bufs=1))
+
+        def load_list(name, src):
+            tile = lists.tile(list(src.shape), U16, name=name)
+            nc.sync.dma_start(tile[:], src)
+            return tile
+
+        def zeroed_plane(name):
+            plane = keep.tile([P, 1024], U8, name=name, align_bytes=64)
+            nc.vector.memset(plane[:].bitcast(I32), 0)
+            return plane
+
+        def load_plane(plane, src):
+            for q in range(4):
+                nc.sync.dma_start(plane[32 * q : 32 * q + 4, :].bitcast(I32), src[0, 4 * q : 4 * q + 4, :].bitcast(I32))
+
+        def load_words(name, src, dtype):
+            tile = keep.tile([P, 1024], dtype, name=name, align_bytes=64)
+            nc.sync.dma_start(tile[:].bitcast(I32), src.bitcast(I32))
+            return tile
+
+        def load_rowwise(name, src):
+            tile = keep.tile([P, PACK], F32, name=name)
+            nc.gpsimd.dma_start(tile[:], src.rearrange("(p t) one -> p (t one)", t=PACK))
+            return tile
+
+        wt_plane = zeroed_plane("wt_plane")
+        xt_plane = zeroed_plane("xt_plane")
+        vs_plane = zeroed_plane("vs_plane")
+        pages = []
+        for u in range(N // P):
+            page = keep.tile([P, E], F32, name="page%d" % u)
+            nc.vector.memset(page[:], 0.0)
+            pages.append(page)
+
+        l1 = load_list("l1", offs)
+        wt_store = load_words("wt_store", wt_words[0], U16)
+        load_plane(wt_plane, wt_scales)
+        l2 = load_list("l2", offs2)
+        xt_store = load_words("xt_store", xt_words[0].rearrange("p n t -> p (n t)"), U32)
+        load_plane(xt_plane, xt_scales)
+        l5 = load_list("l5", offs5)
+        l3 = load_list("l3", offs3)
+        l4 = load_list("l4", offs4)
+        l6 = load_list("l6", offs6)
+        load_plane(vs_plane, vs_scales)
+        vs_store = load_words("vs_store", vs_words[0].rearrange("p n t -> p (n t)"), U32)
+        l7 = load_list("l7", offs7)
+        sg_t = load_rowwise("sg_t", sg)
+        bg_t = load_rowwise("bg_t", bg)
+        sa_t = load_rowwise("sa_t", sa)
+        sb_t = load_rowwise("sb_t", sb)
+
+        wt_pick = keep.tile([P, R], U16, name="wt_pick", align_bytes=64)
+        nc.vector.tensor_copy(wt_pick[:], wt_store[:].indirect(l1[:]))
+        wt_sc = keep.tile([P, PACK, P], U8, name="wt_sc", align_bytes=64)
+        nc.vector.tensor_copy(wt_sc[:].rearrange("p t m -> p m t"), wt_plane[:].indirect(l1[:]))
+        by_slot = wt_pick[:].rearrange("p (m t) -> p t m", t=PACK)
+        wt_dealt = []
+        for t in range(PACK):
+            wt_dealt.append(keep.tile([P, P], U16, name="wt_dealt%d" % t, align_bytes=64))
+        nc.vector.tensor_copy(wt_dealt[0][:], by_slot[:, 0, :])
+        xt_pick = keep.tile([P, J], U32, name="xt_pick", align_bytes=64)
+        nc.vector.tensor_copy(xt_pick[:], xt_store[:].indirect(l2[:]))
+        xt_sc = keep.tile([P, J], U8, name="xt_sc", align_bytes=64)
+        nc.vector.tensor_copy(xt_sc[:], xt_plane[:].indirect(l2[:]))
+        for t in range(1, PACK):
+            nc.vector.tensor_copy(wt_dealt[t][:], by_slot[:, t, :])
+
+        a_rows = []
+        for t in range(PACK):
+            acc = psum.tile([P, J], F32, name="a_acc%d" % t)
+            nc.tensor.matmul_mx(
+                out=acc[:], lhsT=wt_dealt[t][:].bitcast(E2M1X4), lhsT_scale=wt_sc[:, t, :],
+                rhs=xt_pick[:].bitcast(E4M3X4), rhs_scale=xt_sc[:], start=True, stop=True,
+            )
+            rows = keep.tile([P, J], F32, name="a_rows%d" % t)
+            nc.vector.tensor_copy(rows[:], acc[:])
+            a_rows.append(rows)
+
+        vs_pick = keep.tile([P, N], U32, name="vs_pick", align_bytes=64)
+        nc.vector.tensor_copy(vs_pick[:], vs_store[:].indirect(l6[:]))
+        vs_sc = keep.tile([P, N], U8, name="vs_sc", align_bytes=64)
+        nc.vector.tensor_copy(vs_sc[:], vs_plane[:].indirect(l6[:]))
+
+        first = keep.tile([P, PACK, O], F32, name="first")
+        second = keep.tile([P, PACK, O], F32, name="second")
+        gate = keep.tile([P, PACK, O], F32, name="gate")
+        diff = keep.tile([P, PACK, O], F32, name="diff")
+        size = keep.tile([P, PACK, O], F32, name="size")
+        hid = keep.tile([P, O, PACK], BF16, name="hid", align_bytes=64)
+
+        def look_gate(t):
+            nc.scalar.activation(out=gate[:, t, :], in_=a_rows[t][:].indirect(l5[:]), func=ACT.Sigmoid,
+                                 bias=bg_t[:, t : t + 1], scale=sg_t[:, t : t + 1])
+
+        look_gate(0)
+        for t in range(PACK):
+            nc.scalar.activation(out=first[:, t, :], in_=a_rows[t][:].indirect(l3[:]), func=ACT.Copy, scale=sa_t[:, t : t + 1])
+            nc.scalar.activation(out=second[:, t, :], in_=a_rows[t][:].indirect(l4[:]), func=ACT.Copy, scale=sb_t[:, t : t + 1])
+        for t in range(1, PACK):
+            look_gate(t)
+
+        for h in range(2):
+            pair = slice(2 * h, 2 * h + 2)
+            nc.vector.tensor_tensor(diff[:, pair, :], first[:, pair, :], second[:, pair, :], ALU.subtract)
+            nc.vector.scalar_tensor_tensor(size[:, pair, :], diff[:, pair, :], -1.0, diff[:, pair, :], ALU.mult, ALU.max)
+        for h in range(2):
+            pair = slice(2 * h, 2 * h + 2)
+            nc.vector.tensor_tensor(hid[:, :, pair], size[:, pair, :].rearrange("p t o -> p o t"),
+                                    gate[:, pair, :].rearrange("p t o -> p o t"), ALU.mult)
+
+        hid_codes = keep.tile([P, O], U32, name="hid_codes", align_bytes=64)
+        hid_sc = keep.tile([P, O], U8, name="hid_sc", align_bytes=64)
+        nc.vector.quantize_mx(out=hid_codes[:].bitcast(E4M3X4), scales=hid_sc[:], in_=hid[:].rearrange("p o t -> p (o t)"))
+
+        for u in range(N // P):
+            cols = slice(u * P, (u + 1) * P)
+            acc = psum.tile([P, O], F32, name="p_acc%d" % u)
+            nc.tensor.matmul_mx(
+                out=acc[:], lhsT=vs_pick[:, cols].bitcast(E5M2X4), lhsT_scale=vs_sc[:, cols],
+                rhs=hid_codes[:].bitcast(E4M3X4), rhs_scale=hid_sc[:], start=True, stop=True,
+            )
+            vals = keep.tile([P, O], F32, name="p_vals%d" % u)
+            if u == 0:
+                nc.scalar.copy(vals[:], acc[:])
+                nc.scalar.activation(out=pages[u][:].indirect(l7[:]), in_=vals[:], func=ACT.Copy)
+                nc.scalar.dma_start(out[cols, :], pages[u][:])
+            else:
+                nc.vector.tensor_copy(vals[:], acc[:])
+                nc.vector.tensor_copy(pages[u][:].indirect(l7[:]), vals[:])
+                nc.sync.dma_start(out[cols, :], pages[u][:])

@@ -37,21 +37,21 @@ def tile_list_gatedlarger_chosen_store_scattered_kernel(
 
         def zeroed_plane(name):
             plane = keep.tile([P, 1024], U8, name=name, align_bytes=64)
-            nc.vector.memset(plane[:].bitcast(I32), 0)
+            nc.gpsimd.memset(plane[:].bitcast(I32), 0)
             return plane
 
-        def load_plane(plane, src):
+        def load_plane(plane, src, queue):
             for q in range(4):
-                nc.sync.dma_start(plane[32 * q : 32 * q + 4, :].bitcast(I32), src[0, 4 * q : 4 * q + 4, :].bitcast(I32))
+                queue.dma_start(plane[32 * q : 32 * q + 4, :].bitcast(I32), src[0, 4 * q : 4 * q + 4, :].bitcast(I32))
 
         def load_words(name, src, dtype):
             tile = keep.tile([P, 1024], dtype, name=name, align_bytes=64)
             nc.sync.dma_start(tile[:].bitcast(I32), src.bitcast(I32))
             return tile
 
-        def load_rowwise(name, src):
+        def load_rowwise(name, src, queue):
             tile = keep.tile([P, PACK], F32, name=name)
-            nc.gpsimd.dma_start(tile[:], src.rearrange("(p t) one -> p (t one)", t=PACK))
+            queue.dma_start(tile[:], src.rearrange("(p t) one -> p (t one)", t=PACK))
             return tile
 
         wt_plane = zeroed_plane("wt_plane")
@@ -65,80 +65,85 @@ def tile_list_gatedlarger_chosen_store_scattered_kernel(
 
         l1 = load_list("l1", offs)
         wt_store = load_words("wt_store", wt_words[0], U16)
-        load_plane(wt_plane, wt_scales)
+        load_plane(wt_plane, wt_scales, nc.scalar)
         l2 = load_list("l2", offs2)
         xt_store = load_words("xt_store", xt_words[0].rearrange("p n t -> p (n t)"), U32)
-        load_plane(xt_plane, xt_scales)
+        load_plane(xt_plane, xt_scales, nc.scalar)
         l5 = load_list("l5", offs5)
+        sg_t = load_rowwise("sg_t", sg, nc.sync)
         l3 = load_list("l3", offs3)
         l4 = load_list("l4", offs4)
         l6 = load_list("l6", offs6)
-        load_plane(vs_plane, vs_scales)
         vs_store = load_words("vs_store", vs_words[0].rearrange("p n t -> p (n t)"), U32)
+        load_plane(vs_plane, vs_scales, nc.sync)
         l7 = load_list("l7", offs7)
-        sg_t = load_rowwise("sg_t", sg)
-        bg_t = load_rowwise("bg_t", bg)
-        sa_t = load_rowwise("sa_t", sa)
-        sb_t = load_rowwise("sb_t", sb)
+        bg_t = load_rowwise("bg_t", bg, nc.gpsimd)
+        sa_t = load_rowwise("sa_t", sa, nc.gpsimd)
+        sb_t = load_rowwise("sb_t", sb, nc.gpsimd)
 
         wt_pick = keep.tile([P, R], U16, name="wt_pick", align_bytes=64)
         nc.vector.tensor_copy(wt_pick[:], wt_store[:].indirect(l1[:]))
         wt_sc = keep.tile([P, PACK, P], U8, name="wt_sc", align_bytes=64)
         nc.vector.tensor_copy(wt_sc[:].rearrange("p t m -> p m t"), wt_plane[:].indirect(l1[:]))
         by_slot = wt_pick[:].rearrange("p (m t) -> p t m", t=PACK)
-        wt_dealt = []
-        for t in range(PACK):
-            wt_dealt.append(keep.tile([P, P], U16, name="wt_dealt%d" % t, align_bytes=64))
-        nc.vector.tensor_copy(wt_dealt[0][:], by_slot[:, 0, :])
+        wt_lead = keep.tile([P, P], U16, name="wt_lead", align_bytes=64)
+        nc.vector.tensor_copy(wt_lead[:], by_slot[:, 0, :])
         xt_pick = keep.tile([P, J], U32, name="xt_pick", align_bytes=64)
         nc.vector.tensor_copy(xt_pick[:], xt_store[:].indirect(l2[:]))
         xt_sc = keep.tile([P, J], U8, name="xt_sc", align_bytes=64)
-        nc.vector.tensor_copy(xt_sc[:], xt_plane[:].indirect(l2[:]))
-        for t in range(1, PACK):
-            nc.vector.tensor_copy(wt_dealt[t][:], by_slot[:, t, :])
+        for h in range(2):
+            nc.vector.tensor_copy(xt_sc[:, h * P : (h + 1) * P], xt_plane[:].indirect(l2[:, 8 * h : 8 * h + 8]))
+        wt_rest = keep.tile([P, PACK - 1, P], U16, name="wt_rest", tag="xt_plane", align_bytes=64)
+        nc.vector.tensor_copy(wt_rest[:], by_slot[:, 1:, :])
+        wt_dealt = [wt_lead[:]] + [wt_rest[:, t, :] for t in range(PACK - 1)]
 
         a_rows = []
         for t in range(PACK):
-            acc = psum.tile([P, J], F32, name="a_acc%d" % t)
-            nc.tensor.matmul_mx(
-                out=acc[:], lhsT=wt_dealt[t][:].bitcast(E2M1X4), lhsT_scale=wt_sc[:, t, :],
-                rhs=xt_pick[:].bitcast(E4M3X4), rhs_scale=xt_sc[:], start=True, stop=True,
-            )
             rows = keep.tile([P, J], F32, name="a_rows%d" % t)
-            nc.vector.tensor_copy(rows[:], acc[:])
+            width = P if t == 0 else J
+            for c in range(0, J, width):
+                cols = slice(c, c + width)
+                acc = psum.tile([P, width], F32, name="a_acc%d_%d" % (t, c))
+                nc.tensor.matmul_mx(
+                    out=acc[:], lhsT=wt_dealt[t].bitcast(E2M1X4), lhsT_scale=wt_sc[:, t, :],
+                    rhs=xt_pick[:, cols].bitcast(E4M3X4), rhs_scale=xt_sc[:, cols], start=True, stop=True,
+                )
+                nc.vector.tensor_copy(rows[:, cols], acc[:])
             a_rows.append(rows)
 
-        vs_pick = keep.tile([P, N], U32, name="vs_pick", align_bytes=64)
+        vs_pick = keep.tile([P, N], U32, name="vs_pick", tag="xt_pick", align_bytes=64)
         nc.vector.tensor_copy(vs_pick[:], vs_store[:].indirect(l6[:]))
-        vs_sc = keep.tile([P, N], U8, name="vs_sc", align_bytes=64)
+        vs_sc = keep.tile([P, N], U8, name="vs_sc", tag="xt_sc", align_bytes=64)
         nc.vector.tensor_copy(vs_sc[:], vs_plane[:].indirect(l6[:]))
 
         first = keep.tile([P, PACK, O], F32, name="first")
         second = keep.tile([P, PACK, O], F32, name="second")
-        gate = keep.tile([P, PACK, O], F32, name="gate")
+        gate_lead = keep.tile([P, O], F32, name="gate_lead")
         diff = keep.tile([P, PACK, O], F32, name="diff")
         size = keep.tile([P, PACK, O], F32, name="size")
         hid = keep.tile([P, O, PACK], BF16, name="hid", align_bytes=64)
 
-        def look_gate(t):
-            nc.scalar.activation(out=gate[:, t, :], in_=a_rows[t][:].indirect(l5[:]), func=ACT.Sigmoid,
+        def look_gate(t, dst):
+            nc.scalar.activation(out=dst, in_=a_rows[t][:].indirect(l5[:]), func=ACT.Sigmoid,
                                  bias=bg_t[:, t : t + 1], scale=sg_t[:, t : t + 1])
 
-        look_gate(0)
+        look_gate(0, gate_lead[:])
         for t in range(PACK):
             nc.scalar.activation(out=first[:, t, :], in_=a_rows[t][:].indirect(l3[:]), func=ACT.Copy, scale=sa_t[:, t : t + 1])
             nc.scalar.activation(out=second[:, t, :], in_=a_rows[t][:].indirect(l4[:]), func=ACT.Copy, scale=sb_t[:, t : t + 1])
+        gate_rest = keep.tile([P, PACK - 1, O], F32, name="gate_rest", tag="sa_t")
         for t in range(1, PACK):
-            look_gate(t)
+            look_gate(t, gate_rest[:, t - 1, :])
 
-        for h in range(2):
-            pair = slice(2 * h, 2 * h + 2)
+        def magnitude(pair):
             nc.vector.tensor_tensor(diff[:, pair, :], first[:, pair, :], second[:, pair, :], ALU.subtract)
             nc.vector.scalar_tensor_tensor(size[:, pair, :], diff[:, pair, :], -1.0, diff[:, pair, :], ALU.mult, ALU.max)
-        for h in range(2):
-            pair = slice(2 * h, 2 * h + 2)
-            nc.vector.tensor_tensor(hid[:, :, pair], size[:, pair, :].rearrange("p t o -> p o t"),
-                                    gate[:, pair, :].rearrange("p t o -> p o t"), ALU.mult)
+
+        magnitude(slice(0, 2))
+        nc.vector.tensor_tensor(hid[:, :, 0], size[:, 0, :], gate_lead[:], ALU.mult)
+        magnitude(slice(2, 4))
+        nc.vector.tensor_tensor(hid[:, :, 1:], size[:, 1:, :].rearrange("p t o -> p o t"),
+                                gate_rest[:].rearrange("p t o -> p o t"), ALU.mult)
 
         hid_codes = keep.tile([P, O], U32, name="hid_codes", align_bytes=64)
         hid_sc = keep.tile([P, O], U8, name="hid_sc", align_bytes=64)

@@ -37,7 +37,7 @@ def tile_list_gatedlarger_chosen_store_scattered_kernel(
 
         def zeroed_plane(name):
             plane = keep.tile([P, 1024], U8, name=name, align_bytes=64)
-            nc.gpsimd.memset(plane[:].bitcast(I32), 0)
+            nc.vector.memset(plane[:].bitcast(I32), 0)
             return plane
 
         def load_plane(plane, src, queue):
@@ -65,17 +65,17 @@ def tile_list_gatedlarger_chosen_store_scattered_kernel(
 
         l1 = load_list("l1", offs)
         wt_store = load_words("wt_store", wt_words[0], U16)
-        load_plane(wt_plane, wt_scales, nc.scalar)
+        load_plane(wt_plane, wt_scales, nc.sync)
         l2 = load_list("l2", offs2)
         xt_store = load_words("xt_store", xt_words[0].rearrange("p n t -> p (n t)"), U32)
-        load_plane(xt_plane, xt_scales, nc.scalar)
+        load_plane(xt_plane, xt_scales, nc.sync)
         l5 = load_list("l5", offs5)
         sg_t = load_rowwise("sg_t", sg, nc.sync)
         l3 = load_list("l3", offs3)
         l4 = load_list("l4", offs4)
         l6 = load_list("l6", offs6)
-        vs_store = load_words("vs_store", vs_words[0].rearrange("p n t -> p (n t)"), U32)
         load_plane(vs_plane, vs_scales, nc.sync)
+        vs_store = load_words("vs_store", vs_words[0].rearrange("p n t -> p (n t)"), U32)
         l7 = load_list("l7", offs7)
         bg_t = load_rowwise("bg_t", bg, nc.gpsimd)
         sa_t = load_rowwise("sa_t", sa, nc.gpsimd)
@@ -119,8 +119,8 @@ def tile_list_gatedlarger_chosen_store_scattered_kernel(
         first = keep.tile([P, PACK, O], F32, name="first")
         second = keep.tile([P, PACK, O], F32, name="second")
         gate_lead = keep.tile([P, O], F32, name="gate_lead")
-        diff = keep.tile([P, PACK, O], F32, name="diff")
-        size = keep.tile([P, PACK, O], F32, name="size")
+        diff = keep.tile([P, PACK, O], F32, name="diff", tag="vs_store", align_bytes=64)
+        size = keep.tile([P, PACK, O], F32, name="size", tag="vs_plane", align_bytes=64)
         hid = keep.tile([P, O, PACK], BF16, name="hid", align_bytes=64)
 
         def look_gate(t, dst):

from contextlib import ExitStack

import concourse.mybir as mybir

F32 = mybir.dt.float32
BF16 = mybir.dt.bfloat16
I32 = mybir.dt.int32
U32 = mybir.dt.uint32
U16 = mybir.dt.uint16
U8 = mybir.dt.uint8
E4M3X4 = mybir.dt.float8_e4m3fn_x4
E5M2X4 = mybir.dt.float8_e5m2_x4
E2M1X4 = mybir.dt.float4_e2m1fn_x4
ACT = mybir.ActivationFunctionType
ALU = mybir.AluOpType

K, T, J, R, V, O, N, S, E = 512, 1024, 256, 512, 1024, 128, 256, 1024, 1024
P = 128
PACK = 4
FLOPS = 2 * K * R * J + 2 * R * N * O


def tile_list_gatedlarger_chosen_store_scattered_kernel(
    tc, xt_words, xt_scales, wt_words, wt_scales, sa, sb, sg, bg, vs_words, vs_scales,
    offs, offs2, offs3, offs4, offs5, offs6, offs7, out,
):
    nc = tc.nc
    with ExitStack() as ctx:
        lists = ctx.enter_context(tc.tile_pool(name="lists", bufs=1))
        keep = ctx.enter_context(tc.tile_pool(name="keep", bufs=1))
        psum = ctx.enter_context(tc.psum_pool(name="psum", bufs=1))

        def load_list(name, src):
            tile = lists.tile(list(src.shape), U16, name=name)
            nc.sync.dma_start(tile[:], src)
            return tile

        def zeroed_plane(name):
            plane = keep.tile([P, 1024], U8, name=name, align_bytes=64)
            nc.vector.memset(plane[:].bitcast(I32), 0)
            return plane

        def load_plane(plane, src, queue):
            for q in range(4):
                queue.dma_start(plane[32 * q : 32 * q + 4, :].bitcast(I32), src[0, 4 * q : 4 * q + 4, :].bitcast(I32))

        def load_words(name, src, dtype):
            tile = keep.tile([P, 1024], dtype, name=name, align_bytes=64)
            nc.sync.dma_start(tile[:].bitcast(I32), src.bitcast(I32))
            return tile

        def load_rowwise(name, src, queue):
            tile = keep.tile([P, PACK], F32, name=name)
            queue.dma_start(tile[:], src.rearrange("(p t) one -> p (t one)", t=PACK))
            return tile

        wt_plane = zeroed_plane("wt_plane")
        xt_plane = zeroed_plane("xt_plane")
        vs_plane = zeroed_plane("vs_plane")
        pages = []
        for u in range(N // P):
            page = keep.tile([P, E], F32, name="page%d" % u)
            nc.vector.memset(page[:], 0.0)
            pages.append(page)

        l1 = load_list("l1", offs)
        wt_store = load_words("wt_store", wt_words[0], U16)
        load_plane(wt_plane, wt_scales, nc.sync)
        l2 = load_list("l2", offs2)
        xt_store = load_words("xt_store", xt_words[0].rearrange("p n t -> p (n t)"), U32)
        load_plane(xt_plane, xt_scales, nc.sync)
        l5 = load_list("l5", offs5)
        sg_t = load_rowwise("sg_t", sg, nc.sync)
        l3 = load_list("l3", offs3)
        l4 = load_list("l4", offs4)
        l6 = load_list("l6", offs6)
        load_plane(vs_plane, vs_scales, nc.sync)
        vs_store = load_words("vs_store", vs_words[0].rearrange("p n t -> p (n t)"), U32)
        l7 = load_list("l7", offs7)
        bg_t = load_rowwise("bg_t", bg, nc.gpsimd)
        sa_t = load_rowwise("sa_t", sa, nc.gpsimd)
        sb_t = load_rowwise("sb_t", sb, nc.gpsimd)

        wt_pick = keep.tile([P, R], U16, name="wt_pick", align_bytes=64)
        nc.vector.tensor_copy(wt_pick[:], wt_store[:].indirect(l1[:]))
        wt_sc = keep.tile([P, PACK, P], U8, name="wt_sc", align_bytes=64)
        nc.vector.tensor_copy(wt_sc[:].rearrange("p t m -> p m t"), wt_plane[:].indirect(l1[:]))
        by_slot = wt_pick[:].rearrange("p (m t) -> p t m", t=PACK)
        wt_lead = keep.tile([P, P], U16, name="wt_lead", align_bytes=64)
        nc.vector.tensor_copy(wt_lead[:], by_slot[:, 0, :])
        xt_pick = keep.tile([P, J], U32, name="xt_pick", align_bytes=64)
        nc.vector.tensor_copy(xt_pick[:], xt_store[:].indirect(l2[:]))
        xt_sc = keep.tile([P, J], U8, name="xt_sc", align_bytes=64)
        for h in range(2):
            nc.vector.tensor_copy(xt_sc[:, h * P : (h + 1) * P], xt_plane[:].indirect(l2[:, 8 * h : 8 * h + 8]))
        wt_rest = keep.tile([P, PACK - 1, P], U16, name="wt_rest", tag="xt_plane", align_bytes=64)
        nc.vector.tensor_copy(wt_rest[:], by_slot[:, 1:, :])
        wt_dealt = [wt_lead[:]] + [wt_rest[:, t, :] for t in range(PACK - 1)]

        a_rows = []
        for t in range(PACK):
            rows = keep.tile([P, J], F32, name="a_rows%d" % t)
            width = P if t == 0 else J
            for c in range(0, J, width):
                cols = slice(c, c + width)
                acc = psum.tile([P, width], F32, name="a_acc%d_%d" % (t, c))
                nc.tensor.matmul_mx(
                    out=acc[:], lhsT=wt_dealt[t].bitcast(E2M1X4), lhsT_scale=wt_sc[:, t, :],
                    rhs=xt_pick[:, cols].bitcast(E4M3X4), rhs_scale=xt_sc[:, cols], start=True, stop=True,
                )
                nc.vector.tensor_copy(rows[:, cols], acc[:])
            a_rows.append(rows)

        vs_pick = keep.tile([P, N], U32, name="vs_pick", tag="xt_pick", align_bytes=64)
        nc.vector.tensor_copy(vs_pick[:], vs_store[:].indirect(l6[:]))
        vs_sc = keep.tile([P, N], U8, name="vs_sc", tag="xt_sc", align_bytes=64)
        nc.vector.tensor_copy(vs_sc[:], vs_plane[:].indirect(l6[:]))

        first = keep.tile([P, PACK, O], F32, name="first")
        second = keep.tile([P, PACK, O], F32, name="second")
        gate_lead = keep.tile([P, O], F32, name="gate_lead")
        diff = keep.tile([P, PACK, O], F32, name="diff", tag="vs_store", align_bytes=64)
        size = keep.tile([P, PACK, O], F32, name="size", tag="vs_plane", align_bytes=64)
        hid = keep.tile([P, O, PACK], BF16, name="hid", align_bytes=64)

        def look_gate(t, dst):
            nc.scalar.activation(out=dst, in_=a_rows[t][:].indirect(l5[:]), func=ACT.Sigmoid,
                                 bias=bg_t[:, t : t + 1], scale=sg_t[:, t : t + 1])

        look_gate(0, gate_lead[:])
        for t in range(PACK):
            nc.scalar.activation(out=first[:, t, :], in_=a_rows[t][:].indirect(l3[:]), func=ACT.Copy, scale=sa_t[:, t : t + 1])
            nc.scalar.activation(out=second[:, t, :], in_=a_rows[t][:].indirect(l4[:]), func=ACT.Copy, scale=sb_t[:, t : t + 1])
        gate_rest = keep.tile([P, PACK - 1, O], F32, name="gate_rest", tag="sa_t")
        for t in range(1, PACK):
            look_gate(t, gate_rest[:, t - 1, :])

        def magnitude(pair):
            nc.vector.tensor_tensor(diff[:, pair, :], first[:, pair, :], second[:, pair, :], ALU.subtract)
            nc.vector.scalar_tensor_tensor(size[:, pair, :], diff[:, pair, :], -1.0, diff[:, pair, :], ALU.mult, ALU.max)

        magnitude(slice(0, 2))
        nc.vector.tensor_tensor(hid[:, :, 0], size[:, 0, :], gate_lead[:], ALU.mult)
        magnitude(slice(2, 4))
        nc.vector.tensor_tensor(hid[:, :, 1:], size[:, 1:, :].rearrange("p t o -> p o t"),
                                gate_rest[:].rearrange("p t o -> p o t"), ALU.mult)

        hid_codes = keep.tile([P, O], U32, name="hid_codes", align_bytes=64)
        hid_sc = keep.tile([P, O], U8, name="hid_sc", align_bytes=64)
        nc.vector.quantize_mx(out=hid_codes[:].bitcast(E4M3X4), scales=hid_sc[:], in_=hid[:].rearrange("p o t -> p (o t)"))

        for u in range(N // P):
            cols = slice(u * P, (u + 1) * P)
            acc = psum.tile([P, O], F32, name="p_acc%d" % u)
            nc.tensor.matmul_mx(
                out=acc[:], lhsT=vs_pick[:, cols].bitcast(E5M2X4), lhsT_scale=vs_sc[:, cols],
                rhs=hid_codes[:].bitcast(E4M3X4), rhs_scale=hid_sc[:], start=True, stop=True,
            )
            vals = keep.tile([P, O], F32, name="p_vals%d" % u)
            if u == 0:
                nc.scalar.copy(vals[:], acc[:])
                nc.scalar.activation(out=pages[u][:].indirect(l7[:]), in_=vals[:], func=ACT.Copy)
                nc.scalar.dma_start(out[cols, :], pages[u][:])
            else:
                nc.vector.tensor_copy(vals[:], acc[:])
                nc.vector.tensor_copy(pages[u][:].indirect(l7[:]), vals[:])
                nc.sync.dma_start(out[cols, :], pages[u][:])
